import numpy as np
import ml_dtypes


def mxq(x, axis, fmt="e4m3"):
    dtype, down = {"e4m3": (ml_dtypes.float8_e4m3fn, 7), "e5m2": (ml_dtypes.float8_e5m2, 14)}[fmt]
    v = np.moveaxis(np.asarray(x, np.float32).astype(ml_dtypes.bfloat16).astype(np.float64), axis, -1)
    blocks = v.reshape(v.shape[:-1] + (-1, 32))
    amax = np.abs(blocks).max(-1, keepdims=True)
    byte = np.maximum(np.where(amax > 0, np.frexp(amax)[1] - 1 + 127, 0) - down, 1)
    scale = np.exp2(byte - 127.0)
    codes = (blocks / scale).astype(np.float32).astype(dtype).astype(np.float64)
    return np.moveaxis((codes * scale).reshape(v.shape), -1, axis)


WIDE = False


def mx_kscale(k):
    if not WIDE:
        return np.ones(k)
    levels = np.array([10, -10, 5, -5, 0])
    if k % 512:
        return np.exp2(np.random.permutation(np.resize(levels, k // 32))).repeat(32)
    a = np.empty((k // 512, 16))
    for p in range(k // 512):
        a[p, :8] = np.random.permutation(np.resize(levels, 8))
        for g in range(8):
            far = levels[np.abs(levels - a[p, g]) >= 10]
            a[p, g + 8] = far[np.random.randint(len(far))]
    return np.exp2(a.ravel()).repeat(32)


def f64(x):
    return np.asarray(x).astype(np.float64)


def striped(idx):
    return np.tile(idx.reshape(-1, 16).T, (8, 1)).astype(np.uint16)


def unstriped(offs):
    return offs[:16].T.reshape(-1).astype(np.int64)


def striped8(idx):
    return np.concatenate([v.reshape(-1, 16).T for v in idx]).astype(np.uint16)


def unstriped8(offs):
    return np.stack([offs[16 * g:16 * g + 16].T.reshape(-1) for g in range(8)]).astype(np.int64)


E2M1 = np.array([0.0, 0.5, 1.0, 1.5, 2.0, 3.0, 4.0, 6.0, -0.0, -0.5, -1.0, -1.5, -2.0, -3.0, -4.0, -6.0])


def pack_weight(w, fmt):
    k, n = w.shape
    w = f64(np.asarray(w, np.float32).astype(ml_dtypes.bfloat16)).reshape(k // 32, 32, n)
    amax = np.abs(w).max(1)
    if fmt == "e4m3":
        byte = np.frexp(amax)[1] - 1 + 127 - 7
    else:
        mant, ex = np.frexp(amax / 6.0)
        byte = np.where(mant > 0.5, ex, ex - 1) + 127
    byte = np.clip(np.where(amax > 0, byte, 1), 1, 254)
    scaled = (w * np.exp2(127.0 - byte)[:, None, :]).reshape(k, n).astype(np.float32)
    by_word = np.ascontiguousarray(scaled.reshape(k // 512, 128, 4, n).transpose(0, 1, 3, 2))
    if fmt == "e4m3":
        words = by_word.astype(ml_dtypes.float8_e4m3fn).view(np.uint8)
    else:
        c = by_word.astype(ml_dtypes.float4_e2m1fn).view(np.uint8) & 0xF
        words = (c[..., 0::2] | (c[..., 1::2] << 4)).reshape(k // 512, 128, 2 * n)
    return np.ascontiguousarray(words), np.ascontiguousarray(byte.astype(np.uint8).reshape(k // 512, 16, n))


def unpack_weight(words, scales, fmt):
    g, _, n = scales.shape
    words = np.ascontiguousarray(words).reshape(g, 128, n, -1)
    if fmt == "e4m3":
        vals = words.view(ml_dtypes.float8_e4m3fn).astype(np.float64)
    else:
        nib = np.empty((g, 128, n, 4), np.uint8)
        nib[..., 0::2] = words & 0xF
        nib[..., 1::2] = words >> 4
        vals = E2M1[nib]
    vals = vals * np.repeat(np.exp2(scales.astype(np.float64) - 127.0), 8, axis=1)[..., None]
    return vals.transpose(0, 1, 3, 2).reshape(g * 512, n)


def pack_table(v):
    words, scales = pack_weight(v, "e4m3")
    return np.concatenate([words.reshape(words.shape[0], -1), scales.reshape(scales.shape[0], -1)], axis=1)


def unpack_table(tab):
    g, t = tab.shape[0], tab.shape[1] // 528
    return unpack_weight(tab[:, :512 * t].reshape(g, 128, t, 4), tab[:, 512 * t:].reshape(g, 16, t), "e4m3")


def silu(v):
    return v / (1.0 + np.exp(-np.maximum(v, -700.0)))


K, M, T, S = 512, 128, 4096, 2048


def setup_inputs():
    n = np.random.standard_normal
    s = mx_kscale(K)[:, None]
    s2 = mx_kscale(512)[:, None]
    p_w4 = pack_weight(n((K, M)) / np.sqrt(K) / s, "e2m1")
    return {
        "tab": pack_table(n((K, T)) * s),
        "w4_words": p_w4[0],
        "w4_scales": p_w4[1],
        "c": (n((512, S)) * s2).astype(np.float32),
        "u": (n((512, M)) / np.sqrt(512) / s2).astype(np.float32),
        "b": (0.3 * n(128)).astype(np.float32),
        "wgo": np.repeat(np.random.uniform(0.5, 2.0, (8, S)), 16, axis=0).astype(np.float32),
        "offs": striped(np.random.permutation(T)[:S]),
        "offs2": striped8(np.stack([np.random.permutation(T)[:S] for _ in range(8)])),
    }


def reference(tab, w4_words, w4_scales, c, u, b, wgo, offs, offs2):
    tab_ = unpack_table(tab)[:, unstriped(offs)]
    w4_ = unpack_weight(w4_words, w4_scales, "e2m1")
    c_ = mxq(f64(c), 0, "e4m3")
    u_ = mxq(f64(u), 0, "e4m3")
    y = w4_.T @ tab_ + u_.T @ c_
    place = unstriped8(offs2)[np.arange(M) % 128 // 16]
    out = np.zeros((M, T))
    out[np.arange(M)[:, None], place] = f64(wgo)[np.arange(M) % 128] * (silu(y + f64(b)[:, None]))
    return out

@@ -1,0 +1,171 @@
+from contextlib import ExitStack
+
+import concourse.mybir as mybir
+
+K, M, T, S = 512, 128, 4096, 2048
+FLOPS = 2 * 2 * K * M * S
+
+F32 = mybir.dt.float32
+BF16 = mybir.dt.bfloat16
+I32 = mybir.dt.int32
+U32 = mybir.dt.uint32
+U16 = mybir.dt.uint16
+U8 = mybir.dt.uint8
+FP8X4 = mybir.dt.float8_e4m3fn_x4
+FP4X4 = mybir.dt.float4_e2m1fn_x4
+SILU = mybir.ActivationFunctionType.Silu
+MULT = mybir.AluOpType.mult
+
+P = 128
+PACK = 4
+GROUP = 16
+GATHER = 512
+BANK = 512
+FP4_NARROW = 128
+WIDTHS = (256, 256, 512, 512, 512)
+STORES = 2
+
+
+def tile_list_tabhs_d_silu_kernel(tc, tab, w4_words, w4_scales, c, u, b, wgo, offs, offs2, out):
+    nc = tc.nc
+    pieces = len(WIDTHS)
+    first = [sum(WIDTHS[:i]) for i in range(pieces)]
+    gathers = S // GATHER
+    with ExitStack() as ctx:
+        keep = ctx.enter_context(tc.tile_pool(name="keep", bufs=1))
+        psum = ctx.enter_context(tc.psum_pool(name="psum", bufs=1))
+
+        pick = keep.tile([P, S // GROUP], U16, name="pick")
+        place = keep.tile([P, S // GROUP], U16, name="place")
+        tab_scales = keep.tile([P, T // 4], I32, name="tab_scales", align_bytes=64)
+        tab_words = keep.tile([P, T], I32, name="tab_words", align_bytes=64)
+        w4_codes = keep.tile([P, 2 * M // 4], I32, name="w4_codes", align_bytes=64)
+        w4_plane = keep.tile([P, M // 4], I32, name="w4_plane", align_bytes=64)
+        bias = keep.tile([P, 1], F32, name="bias")
+        warm = keep.tile([P, 1], F32, name="warm")
+        warm_out = keep.tile([P, 1], F32, name="warm_out")
+        page = keep.tile([P, T], F32, name="page")
+        u_raw = keep.tile([P, PACK, M], F32, name="u_raw")
+
+        nc.vector.memset(tab_scales[:], 0)
+        nc.vector.memset(warm[:], 0.0)
+        nc.vector.memset(w4_plane[:], 0)
+        nc.vector.memset(page[:], 0.0)
+        nc.scalar.activation(warm_out[:], warm[:], SILU)
+
+        tab_i32 = tab.bitcast(I32)
+        words_hbm = tab_i32[0, 0 : P * T].rearrange("(p t) -> p t", p=P)
+        scales_hbm = tab_i32[0, P * T : P * T + 16 * T // 4].rearrange("(q t) -> q t", q=16)
+        w4_scales_hbm = w4_scales[0].bitcast(I32)
+
+        c_raw = [keep.tile([P, PACK, WIDTHS[i]], F32, name="c_raw%d" % i, tag="stage%d" % i) for i in range(pieces)]
+        weight = [keep.tile([P, WIDTHS[i]], F32, name="weight%d" % i) for i in range(pieces)]
+        c_view = c.rearrange("(p j) s -> p j s", j=PACK)
+
+        def load_c(i):
+            nc.sync.dma_start(c_raw[i][:], c_view[:, :, first[i] : first[i] + WIDTHS[i]])
+
+        def load_weight(i):
+            nc.sync.dma_start(weight[i][:], wgo[:, first[i] : first[i] + WIDTHS[i]])
+
+        nc.sync.dma_start(pick[:], offs)
+        nc.sync.dma_start(w4_codes[:], w4_words[0].bitcast(I32))
+        nc.sync.dma_start(bias[:], b.rearrange("(p o) -> p o", o=1))
+        nc.sync.dma_start(place[:], offs2)
+        for q in range(4):
+            nc.sync.dma_start(tab_scales[32 * q : 32 * q + 4, :], scales_hbm[4 * q : 4 * q + 4, :])
+        nc.sync.dma_start(tab_words[:], words_hbm)
+        nc.sync.dma_start(u_raw[:], u.rearrange("(p j) m -> p j m", j=PACK))
+        load_c(0)
+        for q in range(4):
+            nc.sync.dma_start(w4_plane[32 * q : 32 * q + 4, :], w4_scales_hbm[4 * q : 4 * q + 4, :])
+        load_c(1)
+        for i in range(2, pieces + 2):
+            if i < pieces:
+                load_c(i)
+            load_weight(i - 2)
+
+        got_scales = keep.tile([P, S], U8, name="got_scales", align_bytes=64)
+        nc.vector.tensor_copy(got_scales[:], tab_scales[:].bitcast(U8).indirect(pick[:]))
+
+        got_words = []
+
+        def gather_words(g, tag):
+            words = keep.tile([P, GATHER], U32, name="got_words%d" % g, tag=tag, align_bytes=64)
+            cols = slice(g * GATHER // GROUP, (g + 1) * GATHER // GROUP)
+            nc.vector.tensor_copy(words[:], tab_words[:].bitcast(U32).indirect(pick[:, cols]))
+            got_words.append(words)
+
+        for g in range(gathers - 1):
+            gather_words(g, "got_words%d" % g)
+
+        u_bf = keep.tile([P, M, PACK], BF16, name="u_bf", align_bytes=64)
+        u_codes = keep.tile([P, M], U32, name="u_codes", align_bytes=64)
+        u_plane = keep.tile([P, M], U8, name="u_plane", align_bytes=64)
+        nc.scalar.copy(u_bf[:], u_raw[:].rearrange("p j m -> p m j"))
+        nc.vector.quantize_mx(u_codes[:].bitcast(FP8X4), u_plane[:], u_bf[:].rearrange("p m j -> p (m j)"))
+
+        c_bf = [keep.tile([P, WIDTHS[i], PACK], BF16, name="c_bf%d" % i, tag="c_bf%d" % i, align_bytes=64) for i in range(pieces)]
+        c_codes = [keep.tile([P, WIDTHS[i]], U32, name="c_codes%d" % i, align_bytes=64) for i in range(pieces)]
+        c_plane = [keep.tile([P, WIDTHS[i]], U8, name="c_plane%d" % i, align_bytes=64) for i in range(pieces)]
+        acc = [psum.tile([P, BANK], F32, name="acc%d" % i) for i in range(pieces)]
+        act = []
+        w4_x4 = w4_codes[:].bitcast(U8).bitcast(FP4X4)
+        w4_pl = w4_plane[:].bitcast(U8)
+
+        def cast(i):
+            nc.scalar.copy(
+                c_bf[i][:].rearrange("p (s e) j -> p s j e", e=4),
+                c_raw[i][:].rearrange("p j (s e) -> p s j e", e=4),
+            )
+
+        def quantise(i):
+            nc.vector.quantize_mx(c_codes[i][:].bitcast(FP8X4), c_plane[i][:], c_bf[i][:].rearrange("p s j -> p (s j)"))
+
+        def multiply(i):
+            n = BANK if WIDTHS[i] == BANK else FP4_NARROW
+            for h in range(WIDTHS[i] // n):
+                s0 = first[i] + h * n
+                words = got_words[s0 // GATHER]
+                w0 = s0 % GATHER
+                nc.tensor.matmul_mx(
+                    acc[i][:, h * n : (h + 1) * n],
+                    lhsT=w4_x4,
+                    lhsT_scale=w4_pl,
+                    rhs=words[:, w0 : w0 + n].bitcast(FP8X4),
+                    rhs_scale=got_scales[:, s0 : s0 + n],
+                    start=(h == 0),
+                    stop=False,
+                )
+            nc.tensor.matmul_mx(
+                acc[i][:, 0 : WIDTHS[i]],
+                lhsT=u_codes[:].bitcast(FP8X4),
+                lhsT_scale=u_plane[:],
+                rhs=c_codes[i][:].bitcast(FP8X4),
+                rhs_scale=c_plane[i][:],
+                start=False,
+                stop=True,
+            )
+
+        def activate(i):
+            act.append(keep.tile([P, WIDTHS[i]], F32, name="act%d" % i, tag="stage%d" % (i + 1)))
+            nc.scalar.activation(act[i][:], acc[i][:, 0 : WIDTHS[i]], SILU, bias=bias[:])
+
+        def scatter(i):
+            cols = slice(first[i] // GROUP, (first[i] + WIDTHS[i]) // GROUP)
+            nc.vector.tensor_tensor(page[:].indirect(place[:, cols]), act[i][:], weight[i][:], MULT)
+
+        for i in range(pieces + 1):
+            if i < pieces:
+                cast(i)
+                quantise(i)
+                if i == 0:
+                    gather_words(gathers - 1, "c_bf0")
+                multiply(i)
+            if i >= 1:
+                activate(i - 1)
+                scatter(i - 1)
+
+        for h in range(STORES):
+            cols = slice(h * T // STORES, (h + 1) * T // STORES)
+            nc.sync.dma_start(out[:, cols], page[:, cols])

@@ -19,18 +19,18 @@ MULT = mybir.AluOpType.mult
 P = 128
 PACK = 4
 GROUP = 16
-GATHER = 512
+EARLY = 1536
 BANK = 512
 FP4_NARROW = 128
 WIDTHS = (256, 256, 512, 512, 512)
 STORES = 2
+SCALE_ROW0 = 112
 
 
 def tile_list_tabhs_d_silu_kernel(tc, tab, w4_words, w4_scales, c, u, b, wgo, offs, offs2, out):
     nc = tc.nc
     pieces = len(WIDTHS)
     first = [sum(WIDTHS[:i]) for i in range(pieces)]
-    gathers = S // GATHER
     with ExitStack() as ctx:
         keep = ctx.enter_context(tc.tile_pool(name="keep", bufs=1))
         psum = ctx.enter_context(tc.psum_pool(name="psum", bufs=1))
@@ -47,10 +47,12 @@ def tile_list_tabhs_d_silu_kernel(tc, tab, w4_words, w4_scales, c, u, b, wgo, of
         page = keep.tile([P, T], F32, name="page")
         u_raw = keep.tile([P, PACK, M], F32, name="u_raw")
 
-        nc.vector.memset(tab_scales[:], 0)
-        nc.vector.memset(warm[:], 0.0)
-        nc.vector.memset(w4_plane[:], 0)
-        nc.vector.memset(page[:], 0.0)
+        tab_plane = keep.tile([P, S // 4], I32, name="tab_plane", align_bytes=64)
+        nc.vector.memset(tab_scales[0:SCALE_ROW0, :], 0)
+        nc.vector.memset(tab_plane[:], 0)
+        nc.gpsimd.memset(warm[:], 0.0)
+        nc.gpsimd.memset(w4_plane[:], 0)
+        nc.gpsimd.memset(page[:], 0.0)
         nc.scalar.activation(warm_out[:], warm[:], SILU)
 
         tab_i32 = tab.bitcast(I32)
@@ -69,35 +71,38 @@ def tile_list_tabhs_d_silu_kernel(tc, tab, w4_words, w4_scales, c, u, b, wgo, of
             nc.sync.dma_start(weight[i][:], wgo[:, first[i] : first[i] + WIDTHS[i]])
 
         nc.sync.dma_start(pick[:], offs)
-        nc.sync.dma_start(w4_codes[:], w4_words[0].bitcast(I32))
-        nc.sync.dma_start(bias[:], b.rearrange("(p o) -> p o", o=1))
-        nc.sync.dma_start(place[:], offs2)
-        for q in range(4):
-            nc.sync.dma_start(tab_scales[32 * q : 32 * q + 4, :], scales_hbm[4 * q : 4 * q + 4, :])
+        nc.sync.dma_start(tab_scales[SCALE_ROW0:P, :], scales_hbm)
         nc.sync.dma_start(tab_words[:], words_hbm)
         nc.sync.dma_start(u_raw[:], u.rearrange("(p j) m -> p j m", j=PACK))
-        load_c(0)
         for q in range(4):
             nc.sync.dma_start(w4_plane[32 * q : 32 * q + 4, :], w4_scales_hbm[4 * q : 4 * q + 4, :])
+        load_c(0)
         load_c(1)
-        for i in range(2, pieces + 2):
+
+        got_scales = keep.tile([P, S], U8, name="got_scales", align_bytes=64)
+        nc.vector.tensor_copy(got_scales[:], tab_scales[:].bitcast(U8).indirect(pick[:]))
+        got_rows = got_scales[:].bitcast(I32)
+        for q in range(4):
+            r0 = SCALE_ROW0 + 4 * q
+            nc.sync.dma_start(tab_plane[32 * q : 32 * q + 4, :], got_rows[r0 : r0 + 4, :])
+
+        nc.sync.dma_start(w4_codes[:], w4_words[0].bitcast(I32))
+        nc.sync.dma_start(bias[:], b.rearrange("(p o) -> p o", o=1))
+        load_c(2)
+        nc.sync.dma_start(place[:], offs2)
+        load_weight(0)
+        for i in range(3, pieces + 2):
             if i < pieces:
                 load_c(i)
             load_weight(i - 2)
 
-        got_scales = keep.tile([P, S], U8, name="got_scales", align_bytes=64)
-        nc.vector.tensor_copy(got_scales[:], tab_scales[:].bitcast(U8).indirect(pick[:]))
 
-        got_words = []
+        def gather_words(name, tag, s0, n):
+            words = keep.tile([P, n], U32, name=name, tag=tag, align_bytes=64)
+            nc.vector.tensor_copy(words[:], tab_words[:].bitcast(U32).indirect(pick[:, s0 // GROUP : (s0 + n) // GROUP]))
+            return words
 
-        def gather_words(g, tag):
-            words = keep.tile([P, GATHER], U32, name="got_words%d" % g, tag=tag, align_bytes=64)
-            cols = slice(g * GATHER // GROUP, (g + 1) * GATHER // GROUP)
-            nc.vector.tensor_copy(words[:], tab_words[:].bitcast(U32).indirect(pick[:, cols]))
-            got_words.append(words)
-
-        for g in range(gathers - 1):
-            gather_words(g, "got_words%d" % g)
+        got_words = [gather_words("early_words", "early_words", 0, EARLY)]
 
         u_bf = keep.tile([P, M, PACK], BF16, name="u_bf", align_bytes=64)
         u_codes = keep.tile([P, M], U32, name="u_codes", align_bytes=64)
@@ -126,14 +131,14 @@ def tile_list_tabhs_d_silu_kernel(tc, tab, w4_words, w4_scales, c, u, b, wgo, of
             n = BANK if WIDTHS[i] == BANK else FP4_NARROW
             for h in range(WIDTHS[i] // n):
                 s0 = first[i] + h * n
-                words = got_words[s0 // GATHER]
-                w0 = s0 % GATHER
+                words = got_words[s0 // EARLY]
+                w0 = s0 % EARLY
                 nc.tensor.matmul_mx(
                     acc[i][:, h * n : (h + 1) * n],
                     lhsT=w4_x4,
                     lhsT_scale=w4_pl,
                     rhs=words[:, w0 : w0 + n].bitcast(FP8X4),
-                    rhs_scale=got_scales[:, s0 : s0 + n],
+                    rhs_scale=tab_plane[:].bitcast(U8)[:, s0 : s0 + n],
                     start=(h == 0),
                     stop=False,
                 )
@@ -160,7 +165,7 @@ def tile_list_tabhs_d_silu_kernel(tc, tab, w4_words, w4_scales, c, u, b, wgo, of
                 cast(i)
                 quantise(i)
                 if i == 0:
-                    gather_words(gathers - 1, "c_bf0")
+                    got_words.append(gather_words("late_words", "c_bf0", EARLY, S - EARLY))
                 multiply(i)
             if i >= 1:
                 activate(i - 1)

@@ -42,18 +42,14 @@ def tile_list_tabhs_d_silu_kernel(tc, tab, w4_words, w4_scales, c, u, b, wgo, of
         w4_codes = keep.tile([P, 2 * M // 4], I32, name="w4_codes", align_bytes=64)
         w4_plane = keep.tile([P, M // 4], I32, name="w4_plane", align_bytes=64)
         bias = keep.tile([P, 1], F32, name="bias")
-        warm = keep.tile([P, 1], F32, name="warm")
-        warm_out = keep.tile([P, 1], F32, name="warm_out")
         page = keep.tile([P, T], F32, name="page")
         u_raw = keep.tile([P, PACK, M], F32, name="u_raw")
 
         tab_plane = keep.tile([P, S // 4], I32, name="tab_plane", align_bytes=64)
+        nc.vector.memset(w4_plane[:], 0)
         nc.vector.memset(tab_scales[0:SCALE_ROW0, :], 0)
         nc.vector.memset(tab_plane[:], 0)
-        nc.gpsimd.memset(warm[:], 0.0)
-        nc.gpsimd.memset(w4_plane[:], 0)
-        nc.gpsimd.memset(page[:], 0.0)
-        nc.scalar.activation(warm_out[:], warm[:], SILU)
+        nc.vector.memset(page[:], 0.0)
 
         tab_i32 = tab.bitcast(I32)
         words_hbm = tab_i32[0, 0 : P * T].rearrange("(p t) -> p t", p=P)

@@ -42,14 +42,18 @@ def tile_list_tabhs_d_silu_kernel(tc, tab, w4_words, w4_scales, c, u, b, wgo, of
         w4_codes = keep.tile([P, 2 * M // 4], I32, name="w4_codes", align_bytes=64)
         w4_plane = keep.tile([P, M // 4], I32, name="w4_plane", align_bytes=64)
         bias = keep.tile([P, 1], F32, name="bias")
+        warm = keep.tile([P, 1], F32, name="warm")
+        warm_out = keep.tile([P, 1], F32, name="warm_out")
         page = keep.tile([P, T], F32, name="page")
         u_raw = keep.tile([P, PACK, M], F32, name="u_raw")
 
         tab_plane = keep.tile([P, S // 4], I32, name="tab_plane", align_bytes=64)
         nc.vector.memset(w4_plane[:], 0)
+        nc.vector.memset(warm[:], 0.0)
         nc.vector.memset(tab_scales[0:SCALE_ROW0, :], 0)
         nc.vector.memset(tab_plane[:], 0)
         nc.vector.memset(page[:], 0.0)
+        nc.scalar.activation(warm_out[:], warm[:], SILU)
 
         tab_i32 = tab.bitcast(I32)
         words_hbm = tab_i32[0, 0 : P * T].rearrange("(p t) -> p t", p=P)

from contextlib import ExitStack

import concourse.mybir as mybir

K, M, T, S = 512, 128, 4096, 2048
FLOPS = 2 * 2 * K * M * S

F32 = mybir.dt.float32
BF16 = mybir.dt.bfloat16
I32 = mybir.dt.int32
U32 = mybir.dt.uint32
U16 = mybir.dt.uint16
U8 = mybir.dt.uint8
FP8X4 = mybir.dt.float8_e4m3fn_x4
FP4X4 = mybir.dt.float4_e2m1fn_x4
SILU = mybir.ActivationFunctionType.Silu
MULT = mybir.AluOpType.mult

P = 128
PACK = 4
GROUP = 16
EARLY = 1536
BANK = 512
FP4_NARROW = 128
WIDTHS = (256, 256, 512, 512, 512)
STORES = 2
SCALE_ROW0 = 112


def tile_list_tabhs_d_silu_kernel(tc, tab, w4_words, w4_scales, c, u, b, wgo, offs, offs2, out):
    nc = tc.nc
    pieces = len(WIDTHS)
    first = [sum(WIDTHS[:i]) for i in range(pieces)]
    with ExitStack() as ctx:
        keep = ctx.enter_context(tc.tile_pool(name="keep", bufs=1))
        psum = ctx.enter_context(tc.psum_pool(name="psum", bufs=1))

        pick = keep.tile([P, S // GROUP], U16, name="pick")
        place = keep.tile([P, S // GROUP], U16, name="place")
        tab_scales = keep.tile([P, T // 4], I32, name="tab_scales", align_bytes=64)
        tab_words = keep.tile([P, T], I32, name="tab_words", align_bytes=64)
        w4_codes = keep.tile([P, 2 * M // 4], I32, name="w4_codes", align_bytes=64)
        w4_plane = keep.tile([P, M // 4], I32, name="w4_plane", align_bytes=64)
        bias = keep.tile([P, 1], F32, name="bias")
        warm = keep.tile([P, 1], F32, name="warm")
        warm_out = keep.tile([P, 1], F32, name="warm_out")
        page = keep.tile([P, T], F32, name="page")
        u_raw = keep.tile([P, PACK, M], F32, name="u_raw")

        tab_plane = keep.tile([P, S // 4], I32, name="tab_plane", align_bytes=64)
        nc.vector.memset(w4_plane[:], 0)
        nc.vector.memset(warm[:], 0.0)
        nc.vector.memset(tab_scales[0:SCALE_ROW0, :], 0)
        nc.vector.memset(tab_plane[:], 0)
        nc.vector.memset(page[:], 0.0)
        nc.scalar.activation(warm_out[:], warm[:], SILU)

        tab_i32 = tab.bitcast(I32)
        words_hbm = tab_i32[0, 0 : P * T].rearrange("(p t) -> p t", p=P)
        scales_hbm = tab_i32[0, P * T : P * T + 16 * T // 4].rearrange("(q t) -> q t", q=16)
        w4_scales_hbm = w4_scales[0].bitcast(I32)

        c_raw = [keep.tile([P, PACK, WIDTHS[i]], F32, name="c_raw%d" % i, tag="stage%d" % i) for i in range(pieces)]
        weight = [keep.tile([P, WIDTHS[i]], F32, name="weight%d" % i) for i in range(pieces)]
        c_view = c.rearrange("(p j) s -> p j s", j=PACK)

        def load_c(i):
            nc.sync.dma_start(c_raw[i][:], c_view[:, :, first[i] : first[i] + WIDTHS[i]])

        def load_weight(i):
            nc.sync.dma_start(weight[i][:], wgo[:, first[i] : first[i] + WIDTHS[i]])

        nc.sync.dma_start(pick[:], offs)
        nc.sync.dma_start(tab_scales[SCALE_ROW0:P, :], scales_hbm)
        nc.sync.dma_start(tab_words[:], words_hbm)
        nc.sync.dma_start(u_raw[:], u.rearrange("(p j) m -> p j m", j=PACK))
        for q in range(4):
            nc.sync.dma_start(w4_plane[32 * q : 32 * q + 4, :], w4_scales_hbm[4 * q : 4 * q + 4, :])
        load_c(0)
        load_c(1)

        got_scales = keep.tile([P, S], U8, name="got_scales", align_bytes=64)
        nc.vector.tensor_copy(got_scales[:], tab_scales[:].bitcast(U8).indirect(pick[:]))
        got_rows = got_scales[:].bitcast(I32)
        for q in range(4):
            r0 = SCALE_ROW0 + 4 * q
            nc.sync.dma_start(tab_plane[32 * q : 32 * q + 4, :], got_rows[r0 : r0 + 4, :])

        nc.sync.dma_start(w4_codes[:], w4_words[0].bitcast(I32))
        nc.sync.dma_start(bias[:], b.rearrange("(p o) -> p o", o=1))
        load_c(2)
        nc.sync.dma_start(place[:], offs2)
        load_weight(0)
        for i in range(3, pieces + 2):
            if i < pieces:
                load_c(i)
            load_weight(i - 2)


        def gather_words(name, tag, s0, n):
            words = keep.tile([P, n], U32, name=name, tag=tag, align_bytes=64)
            nc.vector.tensor_copy(words[:], tab_words[:].bitcast(U32).indirect(pick[:, s0 // GROUP : (s0 + n) // GROUP]))
            return words

        got_words = [gather_words("early_words", "early_words", 0, EARLY)]

        u_bf = keep.tile([P, M, PACK], BF16, name="u_bf", align_bytes=64)
        u_codes = keep.tile([P, M], U32, name="u_codes", align_bytes=64)
        u_plane = keep.tile([P, M], U8, name="u_plane", align_bytes=64)
        nc.scalar.copy(u_bf[:], u_raw[:].rearrange("p j m -> p m j"))
        nc.vector.quantize_mx(u_codes[:].bitcast(FP8X4), u_plane[:], u_bf[:].rearrange("p m j -> p (m j)"))

        c_bf = [keep.tile([P, WIDTHS[i], PACK], BF16, name="c_bf%d" % i, tag="c_bf%d" % i, align_bytes=64) for i in range(pieces)]
        c_codes = [keep.tile([P, WIDTHS[i]], U32, name="c_codes%d" % i, align_bytes=64) for i in range(pieces)]
        c_plane = [keep.tile([P, WIDTHS[i]], U8, name="c_plane%d" % i, align_bytes=64) for i in range(pieces)]
        acc = [psum.tile([P, BANK], F32, name="acc%d" % i) for i in range(pieces)]
        act = []
        w4_x4 = w4_codes[:].bitcast(U8).bitcast(FP4X4)
        w4_pl = w4_plane[:].bitcast(U8)

        def cast(i):
            nc.scalar.copy(
                c_bf[i][:].rearrange("p (s e) j -> p s j e", e=4),
                c_raw[i][:].rearrange("p j (s e) -> p s j e", e=4),
            )

        def quantise(i):
            nc.vector.quantize_mx(c_codes[i][:].bitcast(FP8X4), c_plane[i][:], c_bf[i][:].rearrange("p s j -> p (s j)"))

        def multiply(i):
            n = BANK if WIDTHS[i] == BANK else FP4_NARROW
            for h in range(WIDTHS[i] // n):
                s0 = first[i] + h * n
                words = got_words[s0 // EARLY]
                w0 = s0 % EARLY
                nc.tensor.matmul_mx(
                    acc[i][:, h * n : (h + 1) * n],
                    lhsT=w4_x4,
                    lhsT_scale=w4_pl,
                    rhs=words[:, w0 : w0 + n].bitcast(FP8X4),
                    rhs_scale=tab_plane[:].bitcast(U8)[:, s0 : s0 + n],
                    start=(h == 0),
                    stop=False,
                )
            nc.tensor.matmul_mx(
                acc[i][:, 0 : WIDTHS[i]],
                lhsT=u_codes[:].bitcast(FP8X4),
                lhsT_scale=u_plane[:],
                rhs=c_codes[i][:].bitcast(FP8X4),
                rhs_scale=c_plane[i][:],
                start=False,
                stop=True,
            )

        def activate(i):
            act.append(keep.tile([P, WIDTHS[i]], F32, name="act%d" % i, tag="stage%d" % (i + 1)))
            nc.scalar.activation(act[i][:], acc[i][:, 0 : WIDTHS[i]], SILU, bias=bias[:])

        def scatter(i):
            cols = slice(first[i] // GROUP, (first[i] + WIDTHS[i]) // GROUP)
            nc.vector.tensor_tensor(page[:].indirect(place[:, cols]), act[i][:], weight[i][:], MULT)

        for i in range(pieces + 1):
            if i < pieces:
                cast(i)
                quantise(i)
                if i == 0:
                    got_words.append(gather_words("late_words", "c_bf0", EARLY, S - EARLY))
                multiply(i)
            if i >= 1:
                activate(i - 1)
                scatter(i - 1)

        for h in range(STORES):
            cols = slice(h * T // STORES, (h + 1) * T // STORES)
            nc.sync.dma_start(out[:, cols], page[:, cols])
